import numpy as np
import ml_dtypes


def mxq(x, axis, fmt="e4m3"):
    dtype, down = {"e4m3": (ml_dtypes.float8_e4m3fn, 7), "e5m2": (ml_dtypes.float8_e5m2, 14)}[fmt]
    v = np.moveaxis(np.asarray(x, np.float32).astype(ml_dtypes.bfloat16).astype(np.float64), axis, -1)
    blocks = v.reshape(v.shape[:-1] + (-1, 32))
    amax = np.abs(blocks).max(-1, keepdims=True)
    byte = np.maximum(np.where(amax > 0, np.frexp(amax)[1] - 1 + 127, 0) - down, 1)
    scale = np.exp2(byte - 127.0)
    codes = (blocks / scale).astype(np.float32).astype(dtype).astype(np.float64)
    return np.moveaxis((codes * scale).reshape(v.shape), -1, axis)


WIDE = False


def mx_kscale(k):
    if not WIDE:
        return np.ones(k)
    levels = np.array([10, -10, 5, -5, 0])
    if k % 512:
        return np.exp2(np.random.permutation(np.resize(levels, k // 32))).repeat(32)
    a = np.empty((k // 512, 16))
    for p in range(k // 512):
        a[p, :8] = np.random.permutation(np.resize(levels, 8))
        for g in range(8):
            far = levels[np.abs(levels - a[p, g]) >= 10]
            a[p, g + 8] = far[np.random.randint(len(far))]
    return np.exp2(a.ravel()).repeat(32)


def f64(x):
    return np.asarray(x).astype(np.float64)


def striped(idx):
    return np.tile(np.asarray(idx).reshape(-1, 16).T, (8, 1)).astype(np.uint16)


def unstriped(offs):
    return offs[:16].T.reshape(-1).astype(np.int64)


E2M1 = np.array([0.0, 0.5, 1.0, 1.5, 2.0, 3.0, 4.0, 6.0, -0.0, -0.5, -1.0, -1.5, -2.0, -3.0, -4.0, -6.0])


def pack_weight(w, fmt):
    k, n = w.shape
    w = f64(np.asarray(w, np.float32).astype(ml_dtypes.bfloat16)).reshape(k // 32, 32, n)
    amax = np.abs(w).max(1)
    if fmt == "e4m3":
        byte = np.frexp(amax)[1] - 1 + 127 - 7
    else:
        mant, ex = np.frexp(amax / 6.0)
        byte = np.where(mant > 0.5, ex, ex - 1) + 127
    byte = np.clip(np.where(amax > 0, byte, 1), 1, 254)
    scaled = (w * np.exp2(127.0 - byte)[:, None, :]).reshape(k, n).astype(np.float32)
    by_word = np.ascontiguousarray(scaled.reshape(k // 512, 128, 4, n).transpose(0, 1, 3, 2))
    if fmt == "e4m3":
        words = by_word.astype(ml_dtypes.float8_e4m3fn).view(np.uint8)
    else:
        c = by_word.astype(ml_dtypes.float4_e2m1fn).view(np.uint8) & 0xF
        words = (c[..., 0::2] | (c[..., 1::2] << 4)).reshape(k // 512, 128, 2 * n)
    return np.ascontiguousarray(words), np.ascontiguousarray(byte.astype(np.uint8).reshape(k // 512, 16, n))


def unpack_weight(words, scales, fmt):
    g, _, n = scales.shape
    words = np.ascontiguousarray(words).reshape(g, 128, n, -1)
    if fmt == "e4m3":
        vals = words.view(ml_dtypes.float8_e4m3fn).astype(np.float64)
    else:
        nib = np.empty((g, 128, n, 4), np.uint8)
        nib[..., 0::2] = words & 0xF
        nib[..., 1::2] = words >> 4
        vals = E2M1[nib]
    vals = vals * np.repeat(np.exp2(scales.astype(np.float64) - 127.0), 8, axis=1)[..., None]
    return vals.transpose(0, 1, 3, 2).reshape(g * 512, n)


def sigmoid(v):
    return 1.0 / (1.0 + np.exp(-v))


D, E, T, I, Q, G = 512, 512, 2048, 512, 128, 32


def setup_inputs():
    n = np.random.standard_normal
    idx = np.random.permutation(T)[:I]
    fd = mx_kscale(D)
    fe = mx_kscale(E)
    keysp = pack_weight(n((D, T)) / fd[:, None], "e2m1")
    valsp = pack_weight(n((E, T)) / fe[:, None], "e2m1")
    return {
        "query": (n((D, Q)) * 0.8 / np.sqrt(D) * fd[:, None]).astype(np.float32),
        "keys_words": keysp[0],
        "keys_scales": keysp[1],
        "th": (np.random.uniform(-0.5, 0.5, (Q, 1))).astype(np.float32),
        "sharp": (np.random.uniform(1.0, 3.0, (Q, 1))).astype(np.float32),
        "gout": (n((E, Q)) * 1 / np.sqrt(E) * fe[:, None]).astype(np.float32),
        "vals_words": valsp[0],
        "vals_scales": valsp[1],
        "dquery": (n((D, Q)) * 1.0 / np.sqrt(D) * fd[:, None]).astype(np.float32),
        "base": (0.5 * n((Q, T))).astype(np.float32),
        "offs": striped(idx),
    }


def reference(query, keys_words, keys_scales, th, sharp, gout, vals_words, vals_scales, dquery, base, offs):
    idx = unstriped(offs)
    keysu = unpack_weight(keys_words, keys_scales, "e2m1")
    valsu = unpack_weight(vals_words, vals_scales, "e2m1")
    queryq = mxq(f64(query), 0, "e4m3")
    keysidxg = keysu[:, idx]
    a = queryq.T @ keysidxg
    dqueryq = mxq(f64(dquery), 0, "e4m3")
    ta = dqueryq.T @ keysidxg
    s = a.reshape(Q, G, I // G).mean(axis=2) * f64(sharp)
    p = np.exp(s - np.max(s, axis=1, keepdims=True))
    z = np.sum(p, axis=1, keepdims=True)
    r = p / z
    rr = np.repeat(r, I // G, axis=1)
    goutq = mxq(f64(gout), 0, "e4m3")
    valsidxg = valsu[:, idx]
    c0 = goutq.T @ valsidxg
    drr = c0 * sigmoid(a - f64(th))
    dr = drr.reshape(Q, G, I // G).sum(axis=2)
    dz = np.sum(dr * p / np.square(z) * (-1.0), axis=1, keepdims=True)
    dp = dr / z + dz
    ts = ta.reshape(Q, G, I // G).mean(axis=2) * f64(sharp)
    tp = ts * p
    tz = np.sum(tp, axis=1, keepdims=True)
    tr = (tp - tz * p / z) / z
    trr = np.repeat(tr, I // G, axis=1)
    tdrr = ta * sigmoid(a - f64(th)) * (1.0 - sigmoid(a - f64(th))) * c0
    tdr = tdrr.reshape(Q, G, I // G).sum(axis=2)
    tdz = np.sum((tdr * p + tp * dr - tz * z * 2.0 * dr * p / np.square(z)) / np.square(z) * (-1.0), axis=1, keepdims=True)
    tdp = (tdr - tz * dr / z) / z + tdz
    tds = tdp * p + tp * dp
    te1 = tds * f64(sharp) / 16.0
    tr1 = np.repeat(te1, I // G, axis=1)
    tda = (trr * c0 * sigmoid(a - f64(th)) + ta * sigmoid(a - f64(th)) * (1.0 - sigmoid(a - f64(th))) * c0 * rr) * (1.0 - sigmoid(a - f64(th))) + ta * sigmoid(a - f64(th)) * (1.0 - sigmoid(a - f64(th))) * (-1.0) * c0 * rr * sigmoid(a - f64(th)) + tr1
    gs = tda * 32.0
    gf = np.zeros((Q, T))
    gf[:, idx] = gs
    y = f64(base) + gf
    return y

@@ -1,0 +1,164 @@
+from contextlib import ExitStack
+
+import concourse.mybir as mybir
+
+D, E, T, I, Q, G = 512, 512, 2048, 512, 128, 32
+PAGE = I // G
+FLOPS = 3 * 2 * 512 * Q * I
+P = 128
+PACK = 4
+
+F32 = mybir.dt.float32
+BF16 = mybir.dt.bfloat16
+I32 = mybir.dt.int32
+U32 = mybir.dt.uint32
+U16 = mybir.dt.uint16
+U8 = mybir.dt.uint8
+FP8X4 = mybir.dt.float8_e4m3fn_x4
+FP4X4 = mybir.dt.float4_e2m1fn_x4
+ALU = mybir.AluOpType
+ACT = mybir.ActivationFunctionType
+AX = mybir.AxisListType
+
+OUT_CHUNKS = (512, 512, 512, 256, 256)
+
+
+def by_page(ap):
+    return ap.rearrange("p (g j) -> p g j", j=PAGE)
+
+
+def over_page(ap):
+    return ap.unsqueeze(2).to_broadcast([P, G, PAGE])
+
+
+def tile_attend_hvpagetimessigmoid_s_kernel(tc, query, keys_words, keys_scales, th, sharp, gout, vals_words, vals_scales, dquery, base, offs, out):
+    nc = tc.nc
+    with ExitStack() as ctx:
+        sb = ctx.enter_context(tc.tile_pool(name="sb", bufs=1))
+        ps = ctx.enter_context(tc.psum_pool(name="ps", bufs=1))
+
+        def wide(name):
+            return sb.tile([P, I], F32, name=name, align_bytes=64)
+
+        def paged(name):
+            return sb.tile([P, G], F32, name=name, align_bytes=64)
+
+        def column(name):
+            return sb.tile([P, 1], F32, name=name, align_bytes=64)
+
+        offsets = sb.tile([P, I // 16], U16, name="offsets")
+        k_words = sb.tile([P, T], U16, name="k_words", align_bytes=64)
+        k_bytes = sb.tile([P, T], U8, name="k_bytes", align_bytes=64)
+        v_bytes = sb.tile([P, T], U8, name="v_bytes", align_bytes=64)
+        q_raw = sb.tile([P, PACK, Q], F32, name="q_raw", tag="first", align_bytes=64)
+        dq_raw = sb.tile([P, PACK, Q], F32, name="dq_raw", tag="second", align_bytes=64)
+        window = sb.tile([P, T], F32, name="window", align_bytes=64)
+        th_sb, sharp_sb = column("th_sb"), column("sharp_sb")
+
+        nc.vector.memset(k_bytes[:].bitcast(I32), 0)
+        nc.vector.memset(window[:], 0.0)
+        nc.vector.memset(v_bytes[:].bitcast(I32), 0)
+
+        def load_scale_rows(queue, plane, scales):
+            rows = scales[0].bitcast(I32)
+            for quad in range(4):
+                queue.dma_start(out=plane[:].bitcast(I32)[32 * quad : 32 * quad + 4, :], in_=rows[4 * quad : 4 * quad + 4, :])
+
+        nc.sync.dma_start(offsets[:], offs)
+        load_scale_rows(nc.scalar, k_bytes, keys_scales)
+        nc.sync.dma_start(out=k_words[:].bitcast(I32), in_=keys_words[0].bitcast(I32))
+        nc.sync.dma_start(out=q_raw[:], in_=query.rearrange("(p j) w -> p j w", j=PACK))
+        nc.sync.dma_start(out=dq_raw[:], in_=dquery.rearrange("(p j) w -> p j w", j=PACK))
+        nc.gpsimd.dma_start(out=th_sb[:], in_=th)
+        g_raw = sb.tile([P, PACK, Q], F32, name="g_raw", align_bytes=64)
+        nc.gpsimd.dma_start(out=g_raw[:], in_=gout.rearrange("(p j) w -> p j w", j=PACK))
+        nc.gpsimd.dma_start(out=sharp_sb[:], in_=sharp)
+        load_scale_rows(nc.sync, v_bytes, vals_scales)
+
+        neg_half_th, neg_c = column("neg_half_th"), column("neg_c")
+        nc.gpsimd.tensor_scalar(neg_half_th[:], th_sb[:], -0.5, 0.0, ALU.mult, ALU.add)
+        nc.gpsimd.tensor_scalar(neg_c[:], sharp_sb[:], -1.0 / PAGE, 0.0, ALU.mult, ALU.add)
+
+        qq_bf = sb.tile([P, 2, Q, PACK], BF16, name="qq_bf", align_bytes=64)
+        g_bf = sb.tile([P, Q, PACK], BF16, name="g_bf", align_bytes=64)
+        nc.scalar.activation(qq_bf[:, 0], q_raw[:].rearrange("p j w -> p w j"), ACT.Copy)
+        v_words = sb.tile([P, T], U16, name="v_words", tag="first", align_bytes=64)
+        nc.sync.dma_start(out=v_words[:].bitcast(I32), in_=vals_words[0].bitcast(I32))
+        nc.scalar.activation(qq_bf[:, 1], dq_raw[:].rearrange("p j w -> p w j"), ACT.Copy)
+        nc.scalar.activation(g_bf[:], g_raw[:].rearrange("p j w -> p w j"), ACT.Copy)
+        base_sb = sb.tile([P, T], F32, name="base_sb", tag="second", align_bytes=64)
+        nc.sync.dma_start(out=base_sb[:], in_=base)
+
+        kg_words = sb.tile([P, I], U16, name="kg_words", align_bytes=64)
+        kg_bytes = sb.tile([P, I], U8, name="kg_bytes", align_bytes=64)
+        vg_words = sb.tile([P, I], U16, name="vg_words", align_bytes=64)
+        vg_bytes = sb.tile([P, I], U8, name="vg_bytes", align_bytes=64)
+        qq_codes = sb.tile([P, 2 * Q], U32, name="qq_codes", align_bytes=64)
+        qq_scales = sb.tile([P, 2 * Q], U8, name="qq_scales", align_bytes=64)
+        g_codes = sb.tile([P, Q], U32, name="g_codes", align_bytes=64)
+        g_scales = sb.tile([P, Q], U8, name="g_scales", align_bytes=64)
+        a_ps = ps.tile([P, I], F32, name="a_ps")
+        ta_ps = ps.tile([P, I], F32, name="ta_ps")
+        c0_ps = ps.tile([P, I], F32, name="c0_ps")
+
+        nc.vector.tensor_copy(kg_words[:], k_words[:].indirect(offsets[:]))
+        nc.vector.tensor_copy(kg_bytes[:], k_bytes[:].indirect(offsets[:]))
+        nc.vector.quantize_mx(out=qq_codes[:].bitcast(FP8X4), scales=qq_scales[:], in_=qq_bf[:].rearrange("p u w j -> p (u w j)"))
+        for u, acc in enumerate((a_ps, ta_ps)):
+            cols = slice(u * Q, (u + 1) * Q)
+            nc.tensor.matmul_mx(out=acc[:], lhsT=qq_codes[:, cols].bitcast(FP8X4), lhsT_scale=qq_scales[:, cols],
+                                rhs=kg_words[:].bitcast(FP4X4), rhs_scale=kg_bytes[:], start=True, stop=True)
+        nc.vector.tensor_copy(vg_bytes[:], v_bytes[:].indirect(offsets[:]))
+
+        t, t2, y8 = wide("t"), wide("t2"), wide("y8")
+        sum_a, neg_s, p, r = paged("sum_a"), paged("neg_s"), paged("p"), paged("r")
+        neg_max, z, rz = column("neg_max"), column("z"), column("rz")
+        nc.scalar.activation(t[:], a_ps[:], ACT.Tanh, bias=neg_half_th[:], scale=0.5)
+        nc.vector.tensor_reduce(sum_a[:], by_page(a_ps[:]), AX.X, ALU.add)
+        nc.vector.tensor_scalar(neg_s[:], sum_a[:], neg_c[:], None, ALU.mult, ALU.min, accum_out=neg_max[:])
+        nc.scalar.activation(p[:], neg_s[:], ACT.Exp, bias=neg_max[:], scale=-1.0, accum_out=z[:])
+        nc.scalar.activation(t2[:], t[:], ACT.Square)
+
+        sum_ta, neg_rts, neg_e, neg_tr8 = paged("sum_ta"), paged("neg_rts"), paged("neg_e"), paged("neg_tr8")
+        neg_mu = column("neg_mu")
+        nc.vector.tensor_reduce(sum_ta[:], by_page(ta_ps[:]), AX.X, ALU.add)
+        nc.vector.tensor_copy(vg_words[:], v_words[:].indirect(offsets[:]))
+        nc.vector.quantize_mx(out=g_codes[:].bitcast(FP8X4), scales=g_scales[:], in_=g_bf[:].rearrange("p w j -> p (w j)"))
+        nc.tensor.matmul_mx(out=c0_ps[:], lhsT=g_codes[:].bitcast(FP8X4), lhsT_scale=g_scales[:],
+                            rhs=vg_words[:].bitcast(FP4X4), rhs_scale=vg_bytes[:], start=True, stop=True)
+        nc.vector.reciprocal(rz[:], z[:])
+        nc.vector.scalar_tensor_tensor(y8[:], ta_ps[:], 8.0, t[:], ALU.mult, ALU.mult)
+        nc.vector.tensor_scalar(r[:], p[:], rz[:], None, ALU.mult)
+        nc.vector.scalar_tensor_tensor(neg_rts[:], sum_ta[:], neg_c[:], r[:], ALU.mult, ALU.mult, accum_out=neg_mu[:])
+        nc.vector.tensor_scalar(neg_e[:], sum_ta[:], neg_c[:], neg_mu[:], ALU.mult, ALU.subtract)
+        nc.vector.scalar_tensor_tensor(neg_tr8[:], neg_e[:], 8.0, r[:], ALU.mult, ALU.mult)
+
+        zf = wide("zf")
+        for g in range(G):
+            cols = slice(g * PAGE, (g + 1) * PAGE)
+            nc.scalar.activation(zf[:, cols], y8[:, cols], ACT.Identity, bias=neg_tr8[:, g : g + 1], scale=r[:, g : g + 1])
+
+        d2, nu, tt, gm, gm2, spread = wide("d2"), wide("nu"), wide("tt"), wide("gm"), wide("gm2"), wide("spread")
+        sum_d, r_d, nn, sum_t, nw, nk = paged("sum_d"), paged("r_d"), paged("nn"), paged("sum_t"), paged("nw"), paged("nk")
+        m2, ns = column("m2"), column("ns")
+        nc.vector.scalar_tensor_tensor(d2[:], t[:], 1.0, c0_ps[:], ALU.add, ALU.mult)
+        nc.vector.scalar_tensor_tensor(nu[:], t2[:], 1.0, c0_ps[:], ALU.subtract, ALU.mult)
+        nc.vector.tensor_reduce(sum_d[:], by_page(d2[:]), AX.X, ALU.add)
+        nc.vector.tensor_tensor(tt[:], ta_ps[:], nu[:], ALU.mult)
+        nc.vector.scalar_tensor_tensor(r_d[:], sum_d[:], 1.0, r[:], ALU.mult, ALU.mult, accum_out=m2[:])
+        nc.vector.tensor_reduce(sum_t[:], by_page(tt[:]), AX.X, ALU.add)
+        nc.vector.scalar_tensor_tensor(nn[:], sum_d[:], m2[:], neg_e[:], ALU.subtract, ALU.mult)
+        nc.vector.scalar_tensor_tensor(nw[:], sum_t[:], 0.5, nn[:], ALU.mult, ALU.add)
+        nc.vector.tensor_tensor(gm[:], nu[:], zf[:], ALU.mult)
+        nc.vector.scalar_tensor_tensor(nk[:], nw[:], sharp_sb[:], r[:], ALU.mult, ALU.mult, accum_out=ns[:])
+        nc.scalar.activation(by_page(spread[:]), over_page(r[:]), ACT.Copy, scale=ns[:])
+        nc.vector.tensor_tensor(by_page(gm2[:]), by_page(gm[:]), over_page(nk[:]), ALU.subtract)
+        nc.vector.tensor_tensor(window[:].indirect(offsets[:]), gm2[:], spread[:], ALU.add)
+
+        c0 = 0
+        for n, width in enumerate(OUT_CHUNKS):
+            cols = slice(c0, c0 + width)
+            res = sb.tile([P, width], F32, name="res%d" % n, align_bytes=64)
+            nc.vector.tensor_tensor(res[:], window[:, cols], base_sb[:, cols], ALU.add)
+            (nc.sync if n % 2 == 0 else nc.scalar).dma_start(out=out[:, cols], in_=res[:])
+            c0 = c0 + width

@@ -48,16 +48,19 @@ def tile_attend_hvpagetimessigmoid_s_kernel(tc, query, keys_words, keys_scales, 
 
         offsets = sb.tile([P, I // 16], U16, name="offsets")
         k_words = sb.tile([P, T], U16, name="k_words", align_bytes=64)
+        v_words = sb.tile([P, T], U16, name="v_words", align_bytes=64)
         k_bytes = sb.tile([P, T], U8, name="k_bytes", align_bytes=64)
-        v_bytes = sb.tile([P, T], U8, name="v_bytes", align_bytes=64)
-        q_raw = sb.tile([P, PACK, Q], F32, name="q_raw", tag="first", align_bytes=64)
-        dq_raw = sb.tile([P, PACK, Q], F32, name="dq_raw", tag="second", align_bytes=64)
+        v_bytes = sb.tile([P, T], U8, name="v_bytes", tag="after_vb", align_bytes=64)
+        q_raw = sb.tile([P, PACK, Q], F32, name="q_raw", align_bytes=64)
+        dq_raw = sb.tile([P, PACK, Q], F32, name="dq_raw", tag="after_dq", align_bytes=64)
+        g_raw = sb.tile([P, PACK, Q], F32, name="g_raw", tag="after_g", align_bytes=64)
+        base_sb = sb.tile([P, T], F32, name="base_sb", align_bytes=64)
         window = sb.tile([P, T], F32, name="window", align_bytes=64)
         th_sb, sharp_sb = column("th_sb"), column("sharp_sb")
 
         nc.vector.memset(k_bytes[:].bitcast(I32), 0)
-        nc.vector.memset(window[:], 0.0)
         nc.vector.memset(v_bytes[:].bitcast(I32), 0)
+        nc.vector.memset(window[:], 0.0)
 
         def load_scale_rows(queue, plane, scales):
             rows = scales[0].bitcast(I32)
@@ -70,28 +73,26 @@ def tile_attend_hvpagetimessigmoid_s_kernel(tc, query, keys_words, keys_scales, 
         nc.sync.dma_start(out=q_raw[:], in_=query.rearrange("(p j) w -> p j w", j=PACK))
         nc.sync.dma_start(out=dq_raw[:], in_=dquery.rearrange("(p j) w -> p j w", j=PACK))
         nc.gpsimd.dma_start(out=th_sb[:], in_=th)
-        g_raw = sb.tile([P, PACK, Q], F32, name="g_raw", align_bytes=64)
-        nc.gpsimd.dma_start(out=g_raw[:], in_=gout.rearrange("(p j) w -> p j w", j=PACK))
         nc.gpsimd.dma_start(out=sharp_sb[:], in_=sharp)
+        nc.sync.dma_start(out=v_words[:].bitcast(I32), in_=vals_words[0].bitcast(I32))
+        nc.sync.dma_start(out=g_raw[:], in_=gout.rearrange("(p j) w -> p j w", j=PACK))
         load_scale_rows(nc.sync, v_bytes, vals_scales)
+        nc.sync.dma_start(out=base_sb[:], in_=base)
 
-        neg_half_th, neg_c = column("neg_half_th"), column("neg_c")
+        neg_half_th, neg_c, neg_c8 = column("neg_half_th"), column("neg_c"), column("neg_c8")
         nc.gpsimd.tensor_scalar(neg_half_th[:], th_sb[:], -0.5, 0.0, ALU.mult, ALU.add)
         nc.gpsimd.tensor_scalar(neg_c[:], sharp_sb[:], -1.0 / PAGE, 0.0, ALU.mult, ALU.add)
+        nc.gpsimd.tensor_scalar(neg_c8[:], sharp_sb[:], -8.0 / PAGE, 0.0, ALU.mult, ALU.add)
 
         qq_bf = sb.tile([P, 2, Q, PACK], BF16, name="qq_bf", align_bytes=64)
         g_bf = sb.tile([P, Q, PACK], BF16, name="g_bf", align_bytes=64)
         nc.scalar.activation(qq_bf[:, 0], q_raw[:].rearrange("p j w -> p w j"), ACT.Copy)
-        v_words = sb.tile([P, T], U16, name="v_words", tag="first", align_bytes=64)
-        nc.sync.dma_start(out=v_words[:].bitcast(I32), in_=vals_words[0].bitcast(I32))
         nc.scalar.activation(qq_bf[:, 1], dq_raw[:].rearrange("p j w -> p w j"), ACT.Copy)
         nc.scalar.activation(g_bf[:], g_raw[:].rearrange("p j w -> p w j"), ACT.Copy)
-        base_sb = sb.tile([P, T], F32, name="base_sb", tag="second", align_bytes=64)
-        nc.sync.dma_start(out=base_sb[:], in_=base)
 
         kg_words = sb.tile([P, I], U16, name="kg_words", align_bytes=64)
         kg_bytes = sb.tile([P, I], U8, name="kg_bytes", align_bytes=64)
-        vg_words = sb.tile([P, I], U16, name="vg_words", align_bytes=64)
+        vg_words = sb.tile([P, I], U16, name="vg_words", tag="after_dq", align_bytes=64)
         vg_bytes = sb.tile([P, I], U8, name="vg_bytes", align_bytes=64)
         qq_codes = sb.tile([P, 2 * Q], U32, name="qq_codes", align_bytes=64)
         qq_scales = sb.tile([P, 2 * Q], U8, name="qq_scales", align_bytes=64)
@@ -108,52 +109,54 @@ def tile_attend_hvpagetimessigmoid_s_kernel(tc, query, keys_words, keys_scales, 
             cols = slice(u * Q, (u + 1) * Q)
             nc.tensor.matmul_mx(out=acc[:], lhsT=qq_codes[:, cols].bitcast(FP8X4), lhsT_scale=qq_scales[:, cols],
                                 rhs=kg_words[:].bitcast(FP4X4), rhs_scale=kg_bytes[:], start=True, stop=True)
-        nc.vector.tensor_copy(vg_bytes[:], v_bytes[:].indirect(offsets[:]))
+        nc.vector.tensor_copy(vg_words[:], v_words[:].indirect(offsets[:]))
 
-        t, t2, y8 = wide("t"), wide("t2"), wide("y8")
+        t = sb.tile([P, I], F32, name="t", tag="after_g", align_bytes=64)
+        t2 = wide("t2")
         sum_a, neg_s, p, r = paged("sum_a"), paged("neg_s"), paged("p"), paged("r")
-        neg_max, z, rz = column("neg_max"), column("z"), column("rz")
-        nc.scalar.activation(t[:], a_ps[:], ACT.Tanh, bias=neg_half_th[:], scale=0.5)
+        neg_max, z = column("neg_max"), column("z")
         nc.vector.tensor_reduce(sum_a[:], by_page(a_ps[:]), AX.X, ALU.add)
+        nc.scalar.activation(t[:], a_ps[:], ACT.Tanh, bias=neg_half_th[:], scale=0.5)
         nc.vector.tensor_scalar(neg_s[:], sum_a[:], neg_c[:], None, ALU.mult, ALU.min, accum_out=neg_max[:])
         nc.scalar.activation(p[:], neg_s[:], ACT.Exp, bias=neg_max[:], scale=-1.0, accum_out=z[:])
         nc.scalar.activation(t2[:], t[:], ACT.Square)
 
-        sum_ta, neg_rts, neg_e, neg_tr8 = paged("sum_ta"), paged("neg_rts"), paged("neg_e"), paged("neg_tr8")
+        neg_rts, neg_e8, es = paged("neg_rts"), paged("neg_e8"), paged("es")
         neg_mu = column("neg_mu")
-        nc.vector.tensor_reduce(sum_ta[:], by_page(ta_ps[:]), AX.X, ALU.add)
-        nc.vector.tensor_copy(vg_words[:], v_words[:].indirect(offsets[:]))
+        nc.vector.tensor_copy(vg_bytes[:], v_bytes[:].indirect(offsets[:]))
         nc.vector.quantize_mx(out=g_codes[:].bitcast(FP8X4), scales=g_scales[:], in_=g_bf[:].rearrange("p w j -> p (w j)"))
         nc.tensor.matmul_mx(out=c0_ps[:], lhsT=g_codes[:].bitcast(FP8X4), lhsT_scale=g_scales[:],
                             rhs=vg_words[:].bitcast(FP4X4), rhs_scale=vg_bytes[:], start=True, stop=True)
-        nc.vector.reciprocal(rz[:], z[:])
-        nc.vector.scalar_tensor_tensor(y8[:], ta_ps[:], 8.0, t[:], ALU.mult, ALU.mult)
-        nc.vector.tensor_scalar(r[:], p[:], rz[:], None, ALU.mult)
-        nc.vector.scalar_tensor_tensor(neg_rts[:], sum_ta[:], neg_c[:], r[:], ALU.mult, ALU.mult, accum_out=neg_mu[:])
-        nc.vector.tensor_scalar(neg_e[:], sum_ta[:], neg_c[:], neg_mu[:], ALU.mult, ALU.subtract)
-        nc.vector.scalar_tensor_tensor(neg_tr8[:], neg_e[:], 8.0, r[:], ALU.mult, ALU.mult)
+        late = sb.tile([P, I + G + 16], F32, name="late", tag="after_vb", align_bytes=64)
+        y8, sum_ta, rz = late[:, 0:I], late[:, I : I + G], late[:, I + G : I + G + 1]
+        nc.vector.reciprocal(rz, z[:])
+        nc.vector.tensor_reduce(sum_ta, by_page(ta_ps[:]), AX.X, ALU.add)
+        nc.vector.tensor_scalar(r[:], p[:], rz, None, ALU.mult)
+        nc.vector.scalar_tensor_tensor(y8, ta_ps[:], 8.0, t[:], ALU.mult, ALU.mult)
+        nc.vector.scalar_tensor_tensor(neg_rts[:], sum_ta, neg_c8[:], r[:], ALU.mult, ALU.mult, accum_out=neg_mu[:])
+        nc.vector.tensor_scalar(neg_e8[:], sum_ta, neg_c8[:], neg_mu[:], ALU.mult, ALU.subtract)
+        r_wide = wide("r_wide")
+        nc.scalar.activation(by_page(r_wide[:]), over_page(r[:]), ACT.Copy)
 
         zf = wide("zf")
-        for g in range(G):
-            cols = slice(g * PAGE, (g + 1) * PAGE)
-            nc.scalar.activation(zf[:, cols], y8[:, cols], ACT.Identity, bias=neg_tr8[:, g : g + 1], scale=r[:, g : g + 1])
-
-        d2, nu, tt, gm, gm2, spread = wide("d2"), wide("nu"), wide("tt"), wide("gm"), wide("gm2"), wide("spread")
-        sum_d, r_d, nn, sum_t, nw, nk = paged("sum_d"), paged("r_d"), paged("nn"), paged("sum_t"), paged("nw"), paged("nk")
-        m2, ns = column("m2"), column("ns")
+        nc.vector.tensor_tensor(by_page(zf[:]), by_page(y8), over_page(neg_e8[:]), ALU.add)
+        d2, nu, tt, gm, gm2 = wide("d2"), wide("nu"), wide("tt"), wide("gm"), wide("gm2")
+        sum_d, r_d, nn, sum_t, ws = paged("sum_d"), paged("r_d"), paged("nn"), paged("sum_t"), paged("ws")
+        m2, ws_mean = column("m2"), column("ws_mean")
         nc.vector.scalar_tensor_tensor(d2[:], t[:], 1.0, c0_ps[:], ALU.add, ALU.mult)
+        nc.vector.tensor_scalar(es[:], neg_e8[:], neg_c[:], 2.0, ALU.mult, ALU.mult)
         nc.vector.scalar_tensor_tensor(nu[:], t2[:], 1.0, c0_ps[:], ALU.subtract, ALU.mult)
         nc.vector.tensor_reduce(sum_d[:], by_page(d2[:]), AX.X, ALU.add)
         nc.vector.tensor_tensor(tt[:], ta_ps[:], nu[:], ALU.mult)
         nc.vector.scalar_tensor_tensor(r_d[:], sum_d[:], 1.0, r[:], ALU.mult, ALU.mult, accum_out=m2[:])
         nc.vector.tensor_reduce(sum_t[:], by_page(tt[:]), AX.X, ALU.add)
-        nc.vector.scalar_tensor_tensor(nn[:], sum_d[:], m2[:], neg_e[:], ALU.subtract, ALU.mult)
-        nc.vector.scalar_tensor_tensor(nw[:], sum_t[:], 0.5, nn[:], ALU.mult, ALU.add)
+        nc.vector.scalar_tensor_tensor(nn[:], sum_d[:], m2[:], es[:], ALU.subtract, ALU.mult)
+        nc.vector.scalar_tensor_tensor(ws[:], sum_t[:], neg_c8[:], nn[:], ALU.mult, ALU.add)
         nc.vector.tensor_tensor(gm[:], nu[:], zf[:], ALU.mult)
-        nc.vector.scalar_tensor_tensor(nk[:], nw[:], sharp_sb[:], r[:], ALU.mult, ALU.mult, accum_out=ns[:])
-        nc.scalar.activation(by_page(spread[:]), over_page(r[:]), ACT.Copy, scale=ns[:])
-        nc.vector.tensor_tensor(by_page(gm2[:]), by_page(gm[:]), over_page(nk[:]), ALU.subtract)
-        nc.vector.tensor_tensor(window[:].indirect(offsets[:]), gm2[:], spread[:], ALU.add)
+        r_ws = sb.tile([P, G], F32, name="r_ws", tag="after_vb", align_bytes=64)
+        nc.vector.scalar_tensor_tensor(r_ws[:], ws[:], 1.0, r[:], ALU.mult, ALU.mult, accum_out=ws_mean[:])
+        nc.vector.scalar_tensor_tensor(by_page(gm2[:]), by_page(gm[:]), ws_mean[:], over_page(ws[:]), ALU.subtract, ALU.add)
+        nc.vector.tensor_tensor(window[:].indirect(offsets[:]), gm2[:], r_wide[:], ALU.mult)
 
         c0 = 0
         for n, width in enumerate(OUT_CHUNKS):

@@ -60,7 +60,7 @@ def tile_attend_hvpagetimessigmoid_s_kernel(tc, query, keys_words, keys_scales, 
 
         nc.vector.memset(k_bytes[:].bitcast(I32), 0)
         nc.vector.memset(v_bytes[:].bitcast(I32), 0)
-        nc.vector.memset(window[:], 0.0)
+        nc.vector.memset(window[:].bitcast(I32), 0)
 
         def load_scale_rows(queue, plane, scales):
             rows = scales[0].bitcast(I32)
@@ -68,8 +68,8 @@ def tile_attend_hvpagetimessigmoid_s_kernel(tc, query, keys_words, keys_scales, 
                 queue.dma_start(out=plane[:].bitcast(I32)[32 * quad : 32 * quad + 4, :], in_=rows[4 * quad : 4 * quad + 4, :])
 
         nc.sync.dma_start(offsets[:], offs)
-        load_scale_rows(nc.scalar, k_bytes, keys_scales)
         nc.sync.dma_start(out=k_words[:].bitcast(I32), in_=keys_words[0].bitcast(I32))
+        load_scale_rows(nc.sync, k_bytes, keys_scales)
         nc.sync.dma_start(out=q_raw[:], in_=query.rearrange("(p j) w -> p j w", j=PACK))
         nc.sync.dma_start(out=dq_raw[:], in_=dquery.rearrange("(p j) w -> p j w", j=PACK))
         nc.gpsimd.dma_start(out=th_sb[:], in_=th)
@@ -110,51 +110,50 @@ def tile_attend_hvpagetimessigmoid_s_kernel(tc, query, keys_words, keys_scales, 
             nc.tensor.matmul_mx(out=acc[:], lhsT=qq_codes[:, cols].bitcast(FP8X4), lhsT_scale=qq_scales[:, cols],
                                 rhs=kg_words[:].bitcast(FP4X4), rhs_scale=kg_bytes[:], start=True, stop=True)
         nc.vector.tensor_copy(vg_words[:], v_words[:].indirect(offsets[:]))
+        nc.vector.quantize_mx(out=g_codes[:].bitcast(FP8X4), scales=g_scales[:], in_=g_bf[:].rearrange("p w j -> p (w j)"))
 
-        t = sb.tile([P, I], F32, name="t", tag="after_g", align_bytes=64)
-        t2 = wide("t2")
-        sum_a, neg_s, p, r = paged("sum_a"), paged("neg_s"), paged("p"), paged("r")
-        neg_max, z = column("neg_max"), column("z")
+        t, t2 = wide("t"), wide("t2")
+        sum_a = sb.tile([P, G], F32, name="sum_a", tag="after_g", align_bytes=64)
         nc.vector.tensor_reduce(sum_a[:], by_page(a_ps[:]), AX.X, ALU.add)
         nc.scalar.activation(t[:], a_ps[:], ACT.Tanh, bias=neg_half_th[:], scale=0.5)
-        nc.vector.tensor_scalar(neg_s[:], sum_a[:], neg_c[:], None, ALU.mult, ALU.min, accum_out=neg_max[:])
-        nc.scalar.activation(p[:], neg_s[:], ACT.Exp, bias=neg_max[:], scale=-1.0, accum_out=z[:])
         nc.scalar.activation(t2[:], t[:], ACT.Square)
 
-        neg_rts, neg_e8, es = paged("neg_rts"), paged("neg_e8"), paged("es")
-        neg_mu = column("neg_mu")
         nc.vector.tensor_copy(vg_bytes[:], v_bytes[:].indirect(offsets[:]))
-        nc.vector.quantize_mx(out=g_codes[:].bitcast(FP8X4), scales=g_scales[:], in_=g_bf[:].rearrange("p w j -> p (w j)"))
         nc.tensor.matmul_mx(out=c0_ps[:], lhsT=g_codes[:].bitcast(FP8X4), lhsT_scale=g_scales[:],
                             rhs=vg_words[:].bitcast(FP4X4), rhs_scale=vg_bytes[:], start=True, stop=True)
-        late = sb.tile([P, I + G + 16], F32, name="late", tag="after_vb", align_bytes=64)
-        y8, sum_ta, rz = late[:, 0:I], late[:, I : I + G], late[:, I + G : I + G + 1]
-        nc.vector.reciprocal(rz, z[:])
+
+        late = sb.tile([P, I + 2 * G], F32, name="late", tag="after_vb", align_bytes=64)
+        y8, sum_ta, neg_s = late[:, 0:I], late[:, I : I + G], late[:, I + G : I + 2 * G]
+        p, r = paged("p"), paged("r")
+        neg_max, z, rz, neg_mu = column("neg_max"), column("z"), column("rz"), column("neg_mu")
+        neg_rts, neg_e8, es = paged("neg_rts"), paged("neg_e8"), paged("es")
+        nc.vector.tensor_scalar(neg_s, sum_a[:], neg_c[:], None, ALU.mult, ALU.min, accum_out=neg_max[:])
+        nc.scalar.activation(p[:], neg_s, ACT.Exp, bias=neg_max[:], scale=-1.0, accum_out=z[:])
         nc.vector.tensor_reduce(sum_ta, by_page(ta_ps[:]), AX.X, ALU.add)
-        nc.vector.tensor_scalar(r[:], p[:], rz, None, ALU.mult)
         nc.vector.scalar_tensor_tensor(y8, ta_ps[:], 8.0, t[:], ALU.mult, ALU.mult)
+        nc.vector.reciprocal(rz[:], z[:])
+        nc.vector.tensor_scalar(r[:], p[:], rz[:], None, ALU.mult)
         nc.vector.scalar_tensor_tensor(neg_rts[:], sum_ta, neg_c8[:], r[:], ALU.mult, ALU.mult, accum_out=neg_mu[:])
         nc.vector.tensor_scalar(neg_e8[:], sum_ta, neg_c8[:], neg_mu[:], ALU.mult, ALU.subtract)
         r_wide = wide("r_wide")
         nc.scalar.activation(by_page(r_wide[:]), over_page(r[:]), ACT.Copy)
 
-        zf = wide("zf")
-        nc.vector.tensor_tensor(by_page(zf[:]), by_page(y8), over_page(neg_e8[:]), ALU.add)
-        d2, nu, tt, gm, gm2 = wide("d2"), wide("nu"), wide("tt"), wide("gm"), wide("gm2")
-        sum_d, r_d, nn, sum_t, ws = paged("sum_d"), paged("r_d"), paged("nn"), paged("sum_t"), paged("ws")
+        zf, d2, nu, tt, gm, gm2 = wide("zf"), wide("d2"), wide("nu"), wide("tt"), wide("gm"), wide("gm2")
+        sum_d, r_d, nn, sum_t, ws, r_ws = paged("sum_d"), paged("r_d"), paged("nn"), paged("sum_t"), paged("ws"), paged("r_ws")
         m2, ws_mean = column("m2"), column("ws_mean")
-        nc.vector.scalar_tensor_tensor(d2[:], t[:], 1.0, c0_ps[:], ALU.add, ALU.mult)
         nc.vector.tensor_scalar(es[:], neg_e8[:], neg_c[:], 2.0, ALU.mult, ALU.mult)
+        nc.vector.scalar_tensor_tensor(d2[:], t[:], 1.0, c0_ps[:], ALU.add, ALU.mult)
         nc.vector.scalar_tensor_tensor(nu[:], t2[:], 1.0, c0_ps[:], ALU.subtract, ALU.mult)
         nc.vector.tensor_reduce(sum_d[:], by_page(d2[:]), AX.X, ALU.add)
         nc.vector.tensor_tensor(tt[:], ta_ps[:], nu[:], ALU.mult)
         nc.vector.scalar_tensor_tensor(r_d[:], sum_d[:], 1.0, r[:], ALU.mult, ALU.mult, accum_out=m2[:])
-        nc.vector.tensor_reduce(sum_t[:], by_page(tt[:]), AX.X, ALU.add)
+        nc.vector.tensor_tensor(by_page(zf[:]), by_page(y8), over_page(neg_e8[:]), ALU.add)
         nc.vector.scalar_tensor_tensor(nn[:], sum_d[:], m2[:], es[:], ALU.subtract, ALU.mult)
+        nc.vector.tensor_reduce(sum_t[:], by_page(tt[:]), AX.X, ALU.add)
         nc.vector.scalar_tensor_tensor(ws[:], sum_t[:], neg_c8[:], nn[:], ALU.mult, ALU.add)
-        nc.vector.tensor_tensor(gm[:], nu[:], zf[:], ALU.mult)
-        r_ws = sb.tile([P, G], F32, name="r_ws", tag="after_vb", align_bytes=64)
         nc.vector.scalar_tensor_tensor(r_ws[:], ws[:], 1.0, r[:], ALU.mult, ALU.mult, accum_out=ws_mean[:])
+        for cols in (slice(0, I // 2), slice(I // 2, I)):
+            nc.vector.tensor_tensor(gm[:, cols], nu[:, cols], zf[:, cols], ALU.mult)
         nc.vector.scalar_tensor_tensor(by_page(gm2[:]), by_page(gm[:]), ws_mean[:], over_page(ws[:]), ALU.subtract, ALU.add)
         nc.vector.tensor_tensor(window[:].indirect(offsets[:]), gm2[:], r_wide[:], ALU.mult)
 

from contextlib import ExitStack

import concourse.mybir as mybir

D, E, T, I, Q, G = 512, 512, 2048, 512, 128, 32
PAGE = I // G
FLOPS = 3 * 2 * 512 * Q * I
P = 128
PACK = 4

F32 = mybir.dt.float32
BF16 = mybir.dt.bfloat16
I32 = mybir.dt.int32
U32 = mybir.dt.uint32
U16 = mybir.dt.uint16
U8 = mybir.dt.uint8
FP8X4 = mybir.dt.float8_e4m3fn_x4
FP4X4 = mybir.dt.float4_e2m1fn_x4
ALU = mybir.AluOpType
ACT = mybir.ActivationFunctionType
AX = mybir.AxisListType

OUT_CHUNKS = (512, 512, 512, 256, 256)


def by_page(ap):
    return ap.rearrange("p (g j) -> p g j", j=PAGE)


def over_page(ap):
    return ap.unsqueeze(2).to_broadcast([P, G, PAGE])


def tile_attend_hvpagetimessigmoid_s_kernel(tc, query, keys_words, keys_scales, th, sharp, gout, vals_words, vals_scales, dquery, base, offs, out):
    nc = tc.nc
    with ExitStack() as ctx:
        sb = ctx.enter_context(tc.tile_pool(name="sb", bufs=1))
        ps = ctx.enter_context(tc.psum_pool(name="ps", bufs=1))

        def wide(name):
            return sb.tile([P, I], F32, name=name, align_bytes=64)

        def paged(name):
            return sb.tile([P, G], F32, name=name, align_bytes=64)

        def column(name):
            return sb.tile([P, 1], F32, name=name, align_bytes=64)

        offsets = sb.tile([P, I // 16], U16, name="offsets")
        k_words = sb.tile([P, T], U16, name="k_words", align_bytes=64)
        v_words = sb.tile([P, T], U16, name="v_words", align_bytes=64)
        k_bytes = sb.tile([P, T], U8, name="k_bytes", align_bytes=64)
        v_bytes = sb.tile([P, T], U8, name="v_bytes", tag="after_vb", align_bytes=64)
        q_raw = sb.tile([P, PACK, Q], F32, name="q_raw", align_bytes=64)
        dq_raw = sb.tile([P, PACK, Q], F32, name="dq_raw", tag="after_dq", align_bytes=64)
        g_raw = sb.tile([P, PACK, Q], F32, name="g_raw", tag="after_g", align_bytes=64)
        base_sb = sb.tile([P, T], F32, name="base_sb", align_bytes=64)
        window = sb.tile([P, T], F32, name="window", align_bytes=64)
        th_sb, sharp_sb = column("th_sb"), column("sharp_sb")

        nc.vector.memset(k_bytes[:].bitcast(I32), 0)
        nc.vector.memset(v_bytes[:].bitcast(I32), 0)
        nc.vector.memset(window[:].bitcast(I32), 0)

        def load_scale_rows(queue, plane, scales):
            rows = scales[0].bitcast(I32)
            for quad in range(4):
                queue.dma_start(out=plane[:].bitcast(I32)[32 * quad : 32 * quad + 4, :], in_=rows[4 * quad : 4 * quad + 4, :])

        nc.sync.dma_start(offsets[:], offs)
        nc.sync.dma_start(out=k_words[:].bitcast(I32), in_=keys_words[0].bitcast(I32))
        load_scale_rows(nc.sync, k_bytes, keys_scales)
        nc.sync.dma_start(out=q_raw[:], in_=query.rearrange("(p j) w -> p j w", j=PACK))
        nc.sync.dma_start(out=dq_raw[:], in_=dquery.rearrange("(p j) w -> p j w", j=PACK))
        nc.gpsimd.dma_start(out=th_sb[:], in_=th)
        nc.gpsimd.dma_start(out=sharp_sb[:], in_=sharp)
        nc.sync.dma_start(out=v_words[:].bitcast(I32), in_=vals_words[0].bitcast(I32))
        nc.sync.dma_start(out=g_raw[:], in_=gout.rearrange("(p j) w -> p j w", j=PACK))
        load_scale_rows(nc.sync, v_bytes, vals_scales)
        nc.sync.dma_start(out=base_sb[:], in_=base)

        neg_half_th, neg_c, neg_c8 = column("neg_half_th"), column("neg_c"), column("neg_c8")
        nc.gpsimd.tensor_scalar(neg_half_th[:], th_sb[:], -0.5, 0.0, ALU.mult, ALU.add)
        nc.gpsimd.tensor_scalar(neg_c[:], sharp_sb[:], -1.0 / PAGE, 0.0, ALU.mult, ALU.add)
        nc.gpsimd.tensor_scalar(neg_c8[:], sharp_sb[:], -8.0 / PAGE, 0.0, ALU.mult, ALU.add)

        qq_bf = sb.tile([P, 2, Q, PACK], BF16, name="qq_bf", align_bytes=64)
        g_bf = sb.tile([P, Q, PACK], BF16, name="g_bf", align_bytes=64)
        nc.scalar.activation(qq_bf[:, 0], q_raw[:].rearrange("p j w -> p w j"), ACT.Copy)
        nc.scalar.activation(qq_bf[:, 1], dq_raw[:].rearrange("p j w -> p w j"), ACT.Copy)
        nc.scalar.activation(g_bf[:], g_raw[:].rearrange("p j w -> p w j"), ACT.Copy)

        kg_words = sb.tile([P, I], U16, name="kg_words", align_bytes=64)
        kg_bytes = sb.tile([P, I], U8, name="kg_bytes", align_bytes=64)
        vg_words = sb.tile([P, I], U16, name="vg_words", tag="after_dq", align_bytes=64)
        vg_bytes = sb.tile([P, I], U8, name="vg_bytes", align_bytes=64)
        qq_codes = sb.tile([P, 2 * Q], U32, name="qq_codes", align_bytes=64)
        qq_scales = sb.tile([P, 2 * Q], U8, name="qq_scales", align_bytes=64)
        g_codes = sb.tile([P, Q], U32, name="g_codes", align_bytes=64)
        g_scales = sb.tile([P, Q], U8, name="g_scales", align_bytes=64)
        a_ps = ps.tile([P, I], F32, name="a_ps")
        ta_ps = ps.tile([P, I], F32, name="ta_ps")
        c0_ps = ps.tile([P, I], F32, name="c0_ps")

        nc.vector.tensor_copy(kg_words[:], k_words[:].indirect(offsets[:]))
        nc.vector.tensor_copy(kg_bytes[:], k_bytes[:].indirect(offsets[:]))
        nc.vector.quantize_mx(out=qq_codes[:].bitcast(FP8X4), scales=qq_scales[:], in_=qq_bf[:].rearrange("p u w j -> p (u w j)"))
        for u, acc in enumerate((a_ps, ta_ps)):
            cols = slice(u * Q, (u + 1) * Q)
            nc.tensor.matmul_mx(out=acc[:], lhsT=qq_codes[:, cols].bitcast(FP8X4), lhsT_scale=qq_scales[:, cols],
                                rhs=kg_words[:].bitcast(FP4X4), rhs_scale=kg_bytes[:], start=True, stop=True)
        nc.vector.tensor_copy(vg_words[:], v_words[:].indirect(offsets[:]))
        nc.vector.quantize_mx(out=g_codes[:].bitcast(FP8X4), scales=g_scales[:], in_=g_bf[:].rearrange("p w j -> p (w j)"))

        t, t2 = wide("t"), wide("t2")
        sum_a = sb.tile([P, G], F32, name="sum_a", tag="after_g", align_bytes=64)
        nc.vector.tensor_reduce(sum_a[:], by_page(a_ps[:]), AX.X, ALU.add)
        nc.scalar.activation(t[:], a_ps[:], ACT.Tanh, bias=neg_half_th[:], scale=0.5)
        nc.scalar.activation(t2[:], t[:], ACT.Square)

        nc.vector.tensor_copy(vg_bytes[:], v_bytes[:].indirect(offsets[:]))
        nc.tensor.matmul_mx(out=c0_ps[:], lhsT=g_codes[:].bitcast(FP8X4), lhsT_scale=g_scales[:],
                            rhs=vg_words[:].bitcast(FP4X4), rhs_scale=vg_bytes[:], start=True, stop=True)

        late = sb.tile([P, I + 2 * G], F32, name="late", tag="after_vb", align_bytes=64)
        y8, sum_ta, neg_s = late[:, 0:I], late[:, I : I + G], late[:, I + G : I + 2 * G]
        p, r = paged("p"), paged("r")
        neg_max, z, rz, neg_mu = column("neg_max"), column("z"), column("rz"), column("neg_mu")
        neg_rts, neg_e8, es = paged("neg_rts"), paged("neg_e8"), paged("es")
        nc.vector.tensor_scalar(neg_s, sum_a[:], neg_c[:], None, ALU.mult, ALU.min, accum_out=neg_max[:])
        nc.scalar.activation(p[:], neg_s, ACT.Exp, bias=neg_max[:], scale=-1.0, accum_out=z[:])
        nc.vector.tensor_reduce(sum_ta, by_page(ta_ps[:]), AX.X, ALU.add)
        nc.vector.scalar_tensor_tensor(y8, ta_ps[:], 8.0, t[:], ALU.mult, ALU.mult)
        nc.vector.reciprocal(rz[:], z[:])
        nc.vector.tensor_scalar(r[:], p[:], rz[:], None, ALU.mult)
        nc.vector.scalar_tensor_tensor(neg_rts[:], sum_ta, neg_c8[:], r[:], ALU.mult, ALU.mult, accum_out=neg_mu[:])
        nc.vector.tensor_scalar(neg_e8[:], sum_ta, neg_c8[:], neg_mu[:], ALU.mult, ALU.subtract)
        r_wide = wide("r_wide")
        nc.scalar.activation(by_page(r_wide[:]), over_page(r[:]), ACT.Copy)

        zf, d2, nu, tt, gm, gm2 = wide("zf"), wide("d2"), wide("nu"), wide("tt"), wide("gm"), wide("gm2")
        sum_d, r_d, nn, sum_t, ws, r_ws = paged("sum_d"), paged("r_d"), paged("nn"), paged("sum_t"), paged("ws"), paged("r_ws")
        m2, ws_mean = column("m2"), column("ws_mean")
        nc.vector.tensor_scalar(es[:], neg_e8[:], neg_c[:], 2.0, ALU.mult, ALU.mult)
        nc.vector.scalar_tensor_tensor(d2[:], t[:], 1.0, c0_ps[:], ALU.add, ALU.mult)
        nc.vector.scalar_tensor_tensor(nu[:], t2[:], 1.0, c0_ps[:], ALU.subtract, ALU.mult)
        nc.vector.tensor_reduce(sum_d[:], by_page(d2[:]), AX.X, ALU.add)
        nc.vector.tensor_tensor(tt[:], ta_ps[:], nu[:], ALU.mult)
        nc.vector.scalar_tensor_tensor(r_d[:], sum_d[:], 1.0, r[:], ALU.mult, ALU.mult, accum_out=m2[:])
        nc.vector.tensor_tensor(by_page(zf[:]), by_page(y8), over_page(neg_e8[:]), ALU.add)
        nc.vector.scalar_tensor_tensor(nn[:], sum_d[:], m2[:], es[:], ALU.subtract, ALU.mult)
        nc.vector.tensor_reduce(sum_t[:], by_page(tt[:]), AX.X, ALU.add)
        nc.vector.scalar_tensor_tensor(ws[:], sum_t[:], neg_c8[:], nn[:], ALU.mult, ALU.add)
        nc.vector.scalar_tensor_tensor(r_ws[:], ws[:], 1.0, r[:], ALU.mult, ALU.mult, accum_out=ws_mean[:])
        for cols in (slice(0, I // 2), slice(I // 2, I)):
            nc.vector.tensor_tensor(gm[:, cols], nu[:, cols], zf[:, cols], ALU.mult)
        nc.vector.scalar_tensor_tensor(by_page(gm2[:]), by_page(gm[:]), ws_mean[:], over_page(ws[:]), ALU.subtract, ALU.add)
        nc.vector.tensor_tensor(window[:].indirect(offsets[:]), gm2[:], r_wide[:], ALU.mult)

        c0 = 0
        for n, width in enumerate(OUT_CHUNKS):
            cols = slice(c0, c0 + width)
            res = sb.tile([P, width], F32, name="res%d" % n, align_bytes=64)
            nc.vector.tensor_tensor(res[:], window[:, cols], base_sb[:, cols], ALU.add)
            (nc.sync if n % 2 == 0 else nc.scalar).dma_start(out=out[:, cols], in_=res[:])
            c0 = c0 + width
